import numpy as np
import ml_dtypes


def mxq(x, axis, fmt="e4m3"):
    dtype, down = {"e4m3": (ml_dtypes.float8_e4m3fn, 7), "e5m2": (ml_dtypes.float8_e5m2, 14)}[fmt]
    v = np.moveaxis(np.asarray(x, np.float32).astype(ml_dtypes.bfloat16).astype(np.float64), axis, -1)
    blocks = v.reshape(v.shape[:-1] + (-1, 32))
    amax = np.abs(blocks).max(-1, keepdims=True)
    byte = np.maximum(np.where(amax > 0, np.frexp(amax)[1] - 1 + 127, 0) - down, 1)
    scale = np.exp2(byte - 127.0)
    codes = (blocks / scale).astype(np.float32).astype(dtype).astype(np.float64)
    return np.moveaxis((codes * scale).reshape(v.shape), -1, axis)


WIDE = False


def mx_kscale(k):
    if not WIDE:
        return np.ones(k)
    levels = np.array([30, -30])
    if k % 512:
        return np.exp2(np.random.permutation(np.resize(levels, k // 32))).repeat(32)
    a = np.empty((k // 512, 16))
    for p in range(k // 512):
        a[p, :8] = np.random.permutation(np.resize(levels, 8))
        for g in range(8):
            far = levels[np.abs(levels - a[p, g]) >= 10]
            a[p, g + 8] = far[np.random.randint(len(far))]
    return np.exp2(a.ravel()).repeat(32)


def f64(x):
    return np.asarray(x).astype(np.float64)


def striped(idx):
    return np.tile(np.asarray(idx).reshape(-1, 16).T, (8, 1)).astype(np.uint16)


def unstriped(offs):
    return offs[:16].T.reshape(-1).astype(np.int64)


def striped8(idx):
    return np.asarray(idx).reshape(8, -1, 16).transpose(0, 2, 1).reshape(128, -1).astype(np.uint16)


def unstriped8(offs):
    return offs.reshape(8, 16, -1).transpose(0, 2, 1).reshape(8, -1).astype(np.int64)


def pick8(x, idx, run):
    r = np.arange(len(x))
    return x[r[:, None], idx[r % (8 * run) // run]]


E2M1 = np.array([0.0, 0.5, 1.0, 1.5, 2.0, 3.0, 4.0, 6.0, -0.0, -0.5, -1.0, -1.5, -2.0, -3.0, -4.0, -6.0])


def pack_weight(w, fmt):
    k, n = w.shape
    w = f64(np.asarray(w, np.float32).astype(ml_dtypes.bfloat16)).reshape(k // 32, 32, n)
    amax = np.abs(w).max(1)
    if fmt in ("e4m3", "e5m2"):
        byte = np.frexp(amax)[1] - 1 + 127 - (7 if fmt == "e4m3" else 14)
    else:
        mant, ex = np.frexp(amax / 6.0)
        byte = np.where(mant > 0.5, ex, ex - 1) + 127
    byte = np.clip(np.where(amax > 0, byte, 1), 1, 254)
    scaled = (w * np.exp2(127.0 - byte)[:, None, :]).reshape(k, n).astype(np.float32)
    by_word = np.ascontiguousarray(scaled.reshape(k // 512, 128, 4, n).transpose(0, 1, 3, 2))
    if fmt in ("e4m3", "e5m2"):
        words = by_word.astype(ml_dtypes.float8_e4m3fn if fmt == "e4m3" else ml_dtypes.float8_e5m2).view(np.uint8)
    else:
        c = by_word.astype(ml_dtypes.float4_e2m1fn).view(np.uint8) & 0xF
        words = (c[..., 0::2] | (c[..., 1::2] << 4)).reshape(k // 512, 128, 2 * n)
    return np.ascontiguousarray(words), np.ascontiguousarray(byte.astype(np.uint8).reshape(k // 512, 16, n))


def unpack_weight(words, scales, fmt):
    g, _, n = scales.shape
    words = np.ascontiguousarray(words).reshape(g, 128, n, -1)
    if fmt in ("e4m3", "e5m2"):
        vals = words.view(ml_dtypes.float8_e4m3fn if fmt == "e4m3" else ml_dtypes.float8_e5m2).astype(np.float64)
    else:
        nib = np.empty((g, 128, n, 4), np.uint8)
        nib[..., 0::2] = words & 0xF
        nib[..., 1::2] = words >> 4
        vals = E2M1[nib]
    vals = vals * np.repeat(np.exp2(scales.astype(np.float64) - 127.0), 8, axis=1)[..., None]
    return vals.transpose(0, 1, 3, 2).reshape(g * 512, n)


def bf(x):
    return np.asarray(x, np.float32).astype(ml_dtypes.bfloat16)


def planes(Y):
    r, m = Y.shape
    b = f64(bf(Y)).reshape(r // 32, 32, m)
    amax = np.abs(b).max(1)
    byte = np.clip(np.where(amax > 0, np.frexp(amax)[1] - 1 + 127 - 7, 1), 1, 254)
    codes = (b * np.exp2(127.0 - byte)[:, None, :]).reshape(r, m).astype(np.float32).astype(ml_dtypes.float8_e4m3fn).view(np.uint8)
    words = codes.reshape(r // 512, 128, 4, m).transpose(0, 1, 3, 2)
    return np.ascontiguousarray(words), np.ascontiguousarray(byte.astype(np.uint8).reshape(r // 512, 16, m))


K, T, J, R, G, N, C = 1024, 512, 256, 512, 128, 512, 1024


def setup_inputs():
    n = np.random.standard_normal
    idx = np.stack([np.random.permutation(T)[:J] for _ in range(8)])
    idx2 = np.random.permutation(C)[:G]
    fk = mx_kscale(K)
    fr = mx_kscale(R)
    xtp = pack_weight(n((K, T)) / fk[:, None], "e5m2")
    wp = pack_weight(n((K, R)) * 1 / np.sqrt(K) * fk[:, None] * fr, "e4m3")
    wbp = pack_weight(n((R, N)) * 1 / np.sqrt(R) / fr[:, None], "e2m1")
    return {
        "xt_words": xtp[0],
        "xt_scales": xtp[1],
        "w_words": wp[0],
        "w_scales": wp[1],
        "wb_words": wbp[0],
        "wb_scales": wbp[1],
        "old": (1.0 * n((N, C))).astype(np.float32),
        "offs": striped8(idx),
        "offs2": striped(idx2),
    }


def reference(xt_words, xt_scales, w_words, w_scales, wb_words, wb_scales, old, offs, offs2):
    idx = unstriped8(offs)
    idx2 = unstriped(offs2)
    xtu = unpack_weight(xt_words, xt_scales, "e5m2")
    wu = unpack_weight(w_words, w_scales, "e4m3")
    wbu = unpack_weight(wb_words, wb_scales, "e2m1")
    xtidxg = pick8(xtu, idx, 64)
    a = wu.T @ xtidxg
    hid = a.reshape(R, G, J // G).max(axis=2)
    hidq = mxq(hid, 0, "e5m2")
    p = wbu.T @ hidq
    pp = np.zeros((N, C))
    pp[:, idx2] = p
    y = pp + 0.5 * f64(old)
    words, scales = planes(y)
    return y, words, scales

@@ -1,0 +1,190 @@
+from contextlib import ExitStack
+
+import concourse.mybir as mybir
+
+K, T, J, R, G, N, C = 1024, 512, 256, 512, 128, 512, 1024
+FLOPS = 2 * K * R * J + 2 * R * N * G
+
+F32 = mybir.dt.float32
+BF16 = mybir.dt.bfloat16
+I32 = mybir.dt.int32
+U32 = mybir.dt.uint32
+U16 = mybir.dt.uint16
+U8 = mybir.dt.uint8
+E4M3X4 = mybir.dt.float8_e4m3fn_x4
+E5M2X4 = mybir.dt.float8_e5m2_x4
+E2M1X4 = mybir.dt.float4_e2m1fn_x4
+ALU = mybir.AluOpType
+COPY = mybir.ActivationFunctionType.Copy
+
+P = 128
+PACK = 4
+PASSES = K // (P * PACK)
+QUADS = 4
+CHUNK = 256
+ROUND_ON_VECTOR = (2,)
+
+
+def tile_list_headpicks_pooled_scattered_pl_kernel(
+    tc, xt_words, xt_scales, w_words, w_scales, wb_words, wb_scales, old, offs, offs2, out_0, out_1, out_2
+):
+    nc = tc.nc
+    with ExitStack() as ctx:
+        keep = ctx.enter_context(tc.tile_pool(name="keep", bufs=1))
+        psum = ctx.enter_context(tc.psum_pool(name="psum", bufs=1))
+
+        picks = keep.tile([P, J // 16], U16, name="picks")
+        nc.sync.dma_start(picks[:], offs)
+
+        xs_win = [keep.tile([P, T], U8, name=f"xs_win{z}", tag=f"xs_win{z}", align_bytes=64) for z in range(PASSES)]
+        for z in range(PASSES):
+            nc.vector.memset(xs_win[z][:].bitcast(I32), 0)
+            nc.sync.dma_start(xs_win[z][0:P:8, :].bitcast(I32), xt_scales[z].bitcast(I32))
+        xw_win = [keep.tile([P, T], U32, name=f"xw_win{z}", tag=f"xw_win{z}", align_bytes=64) for z in range(PASSES)]
+        for z in range(PASSES):
+            nc.sync.dma_start(xw_win[z][:].bitcast(I32), xt_words[z].rearrange("p c r -> p (c r)").bitcast(I32))
+        w_raw = keep.tile([P, PASSES, R], I32, name="w_raw", tag="w_raw", align_bytes=64)
+        nc.sync.dma_start(w_raw[:], w_words.rearrange("z p c r -> p z (c r)").bitcast(I32))
+        ws_raw = keep.tile([P, PASSES, R], U8, name="ws_raw", tag="ws_raw", align_bytes=64)
+        nc.vector.memset(ws_raw[:].bitcast(I32), 0)
+        for q in range(QUADS):
+            nc.scalar.dma_start(
+                ws_raw[32 * q : 32 * q + 4].bitcast(I32),
+                w_scales[:, 4 * q : 4 * q + 4, :].rearrange("z r c -> r z c").bitcast(I32),
+            )
+        places = keep.tile([P, G // 16], U16, name="places")
+        nc.sync.dma_start(places[:], offs2)
+
+        xs_plane = keep.tile([P, PASSES * J], U8, name="xs_plane", align_bytes=64)
+        nc.vector.memset(xs_plane[:].bitcast(I32), 0)
+
+        xs_got = keep.tile([P, PASSES * J], U8, name="xs_got", tag="xs_got", align_bytes=64)
+        for z in range(PASSES):
+            nc.vector.tensor_copy(xs_got[:, z * J : (z + 1) * J], xs_win[z][:].indirect(picks[:]))
+        for r in range(4):
+            queue = nc.sync if r % 2 == 0 else nc.scalar
+            queue.dma_start(xs_plane[r:P:32, :].bitcast(I32), xs_got[8 * r : P : 32, :].bitcast(I32))
+
+        xw_got = keep.tile([P, PASSES * J], U32, name="xw_got", tag="xs_win1", align_bytes=64)
+        for z in range(PASSES):
+            nc.vector.tensor_copy(xw_got[:, z * J : (z + 1) * J], xw_win[z][:].indirect(picks[:]))
+
+        w_dealt = keep.tile([P, PASSES, PACK, P], I32, name="w_dealt", align_bytes=64)
+        nc.vector.tensor_copy(
+            w_dealt[:].rearrange("p z t m -> p z m t"), w_raw[:].rearrange("p z (m t) -> p z m t", t=PACK)
+        )
+        ws_dealt = keep.tile([P, PASSES, PACK, P], U8, name="ws_dealt", align_bytes=64)
+        nc.vector.tensor_copy(
+            ws_dealt[:].rearrange("p z t m -> p z m t"), ws_raw[:].rearrange("p z (m t) -> p z m t", t=PACK)
+        )
+
+        wb_raw = keep.tile([P, 2 * N], U8, name="wb_raw", tag="xw_win0", align_bytes=64)
+        nc.sync.dma_start(wb_raw[:].bitcast(I32), wb_words[0].bitcast(I32))
+        wbs_raw = keep.tile([P, N], U8, name="wbs_raw", tag="xw_win1", align_bytes=64)
+        nc.vector.memset(wbs_raw[:].bitcast(I32), 0)
+        for q in range(QUADS):
+            nc.sync.dma_start(wbs_raw[32 * q : 32 * q + 4, :].bitcast(I32), wb_scales[0, 4 * q : 4 * q + 4, :].bitcast(I32))
+        old_rows = old.rearrange("(p t) c -> p t c", t=PACK)
+        old_sb = []
+        for h in range(2):
+            half = keep.tile([P, 2, C], F32, name=f"old{h}", tag=("w_raw", "ws_raw")[h], align_bytes=64)
+            nc.sync.dma_start(half[:], old_rows[:, 2 * h : 2 * h + 2, :])
+            old_sb.append(half)
+
+        hid = keep.tile([P, G, PACK], BF16, name="hid", align_bytes=64)
+        for h in range(2):
+            bank = psum.tile([P, 2, J], F32, name=f"a{h}")
+            for u in range(2):
+                t = 2 * h + u
+                for z in range(PASSES):
+                    nc.tensor.matmul_mx(
+                        out=bank[:, u, :],
+                        lhsT=w_dealt[:, z, t, :].bitcast(E4M3X4),
+                        lhsT_scale=ws_dealt[:, z, t, :],
+                        rhs=xw_got[:, z * J : (z + 1) * J].bitcast(E5M2X4),
+                        rhs_scale=xs_plane[:, z * J : (z + 1) * J],
+                        start=(z == 0),
+                        stop=(z == PASSES - 1),
+                    )
+            nc.vector.tensor_reduce(
+                hid[:, :, 2 * h : 2 * h + 2],
+                bank[:].rearrange("p u (g two) -> p g u two", two=2),
+                axis=mybir.AxisListType.X,
+                op=ALU.max,
+            )
+
+        wb_dealt = keep.tile([P, PACK, 2 * P], U8, name="wb_dealt", align_bytes=64)
+        nc.vector.tensor_copy(
+            wb_dealt[:].bitcast(U16).rearrange("p t m -> p m t"),
+            wb_raw[:].bitcast(U16).rearrange("p (m t) -> p m t", t=PACK),
+        )
+        wbs_dealt = keep.tile([P, PACK, P], U8, name="wbs_dealt", align_bytes=64)
+        nc.vector.tensor_copy(
+            wbs_dealt[:].rearrange("p t m -> p m t"), wbs_raw[:].rearrange("p (m t) -> p m t", t=PACK)
+        )
+
+        pages = [keep.tile([P, C], F32, name=f"page{t}", tag=("page0", "page1", "page2", "xs_got")[t], align_bytes=64) for t in range(PACK)]
+        for t in range(PACK):
+            nc.vector.memset(pages[t][:].bitcast(I32), 0)
+
+        hid_words = keep.tile([P, G], U32, name="hid_words", align_bytes=64)
+        hid_plane = keep.tile([P, G], U8, name="hid_plane", align_bytes=64)
+        nc.vector.quantize_mx(
+            out=hid_words[:].bitcast(E5M2X4), scales=hid_plane[:], in_=hid[:].rearrange("p g t -> p (g t)")
+        )
+
+        for t in range(PACK):
+            bank = psum.tile([P, G], F32, name=f"p{t}")
+            nc.tensor.matmul_mx(
+                out=bank[:],
+                lhsT=wb_dealt[:, t, :].bitcast(E2M1X4),
+                lhsT_scale=wbs_dealt[:, t, :],
+                rhs=hid_words[:].bitcast(E5M2X4),
+                rhs_scale=hid_plane[:],
+                start=True,
+                stop=True,
+            )
+            p_sb = keep.tile([P, G], F32, name=f"p_sb{t}")
+            if t == 0:
+                nc.vector.tensor_copy(p_sb[:], bank[:])
+                nc.vector.tensor_copy(pages[t][:].indirect(places[:]), p_sb[:])
+            else:
+                nc.scalar.activation(p_sb[:], bank[:], COPY)
+                nc.scalar.activation(pages[t][:].indirect(places[:]), p_sb[:], COPY)
+
+        y = keep.tile([P, PACK, C], F32, name="y", align_bytes=64)
+        y_rows = out_0.rearrange("(p t) c -> p t c", t=PACK)
+
+        def add_old(t, cols):
+            nc.vector.scalar_tensor_tensor(
+                out=y[:, t, cols], in0=old_sb[t // 2][:, t % 2, cols], scalar=0.5, in1=pages[t][:, cols],
+                op0=ALU.mult, op1=ALU.add,
+            )
+
+        for t in range(2):
+            add_old(t, slice(0, C))
+            nc.sync.dma_start(y_rows[:, t, :], y[:, t, :])
+
+        y_words = keep.tile([P, C], U32, name="y_words", align_bytes=64)
+        y_plane = keep.tile([P, C], U8, name="y_plane", align_bytes=64)
+        words_out = out_1[0].rearrange("p c r -> p (c r)").bitcast(I32)
+        chunks = [slice(c, c + CHUNK) for c in range(0, C, CHUNK)]
+        for cols in chunks:
+            for t in range(2, PACK):
+                add_old(t, cols)
+            nc.sync.dma_start(y_rows[:, 2:PACK, cols], y[:, 2:PACK, cols])
+        for i, cols in enumerate(chunks):
+            y16 = keep.tile([P, CHUNK, PACK], BF16, name=f"y16_{i}", align_bytes=64)
+            dst = y16[:].rearrange("p (c i) t -> p c t i", i=4)
+            src = y[:, :, cols].rearrange("p t (c i) -> p c t i", i=4)
+            if i in ROUND_ON_VECTOR:
+                nc.vector.tensor_copy(dst, src)
+            else:
+                nc.scalar.copy(dst, src)
+            nc.vector.quantize_mx(
+                out=y_words[:, cols].bitcast(E4M3X4), scales=y_plane[:, cols], in_=y16[:].rearrange("p c t -> p (c t)")
+            )
+            nc.sync.dma_start(words_out[:, cols], y_words[:, cols].bitcast(I32))
+        for q in range(QUADS):
+            queue = nc.sync if q % 2 == 0 else nc.scalar
+            queue.dma_start(out_2[0, 4 * q : 4 * q + 4, :].bitcast(I32), y_plane[32 * q : 32 * q + 4, :].bitcast(I32))

@@ -22,7 +22,6 @@ PACK = 4
 PASSES = K // (P * PACK)
 QUADS = 4
 CHUNK = 256
-ROUND_ON_VECTOR = (2,)
 
 
 def tile_list_headpicks_pooled_scattered_pl_kernel(
@@ -52,8 +51,6 @@ def tile_list_headpicks_pooled_scattered_pl_kernel(
                 ws_raw[32 * q : 32 * q + 4].bitcast(I32),
                 w_scales[:, 4 * q : 4 * q + 4, :].rearrange("z r c -> r z c").bitcast(I32),
             )
-        places = keep.tile([P, G // 16], U16, name="places")
-        nc.sync.dma_start(places[:], offs2)
 
         xs_plane = keep.tile([P, PASSES * J], U8, name="xs_plane", align_bytes=64)
         nc.vector.memset(xs_plane[:].bitcast(I32), 0)
@@ -66,73 +63,73 @@ def tile_list_headpicks_pooled_scattered_pl_kernel(
             queue.dma_start(xs_plane[r:P:32, :].bitcast(I32), xs_got[8 * r : P : 32, :].bitcast(I32))
 
         xw_got = keep.tile([P, PASSES * J], U32, name="xw_got", tag="xs_win1", align_bytes=64)
+        w_dealt = keep.tile([P, PASSES, PACK, P], I32, name="w_dealt", align_bytes=64)
+        ws_dealt = keep.tile([P, PASSES, PACK, P], U8, name="ws_dealt", align_bytes=64)
         for z in range(PASSES):
             nc.vector.tensor_copy(xw_got[:, z * J : (z + 1) * J], xw_win[z][:].indirect(picks[:]))
+            for dealt, raw in ((w_dealt, w_raw), (ws_dealt, ws_raw)):
+                nc.vector.tensor_copy(
+                    dealt[:, z].rearrange("p t m -> p m t"), raw[:, z].rearrange("p (m t) -> p m t", t=PACK)
+                )
 
-        w_dealt = keep.tile([P, PASSES, PACK, P], I32, name="w_dealt", align_bytes=64)
-        nc.vector.tensor_copy(
-            w_dealt[:].rearrange("p z t m -> p z m t"), w_raw[:].rearrange("p z (m t) -> p z m t", t=PACK)
-        )
-        ws_dealt = keep.tile([P, PASSES, PACK, P], U8, name="ws_dealt", align_bytes=64)
-        nc.vector.tensor_copy(
-            ws_dealt[:].rearrange("p z t m -> p z m t"), ws_raw[:].rearrange("p z (m t) -> p z m t", t=PACK)
-        )
-
-        wb_raw = keep.tile([P, 2 * N], U8, name="wb_raw", tag="xw_win0", align_bytes=64)
-        nc.sync.dma_start(wb_raw[:].bitcast(I32), wb_words[0].bitcast(I32))
-        wbs_raw = keep.tile([P, N], U8, name="wbs_raw", tag="xw_win1", align_bytes=64)
+        wb_raw = keep.tile([P, 2 * N], U8, name="wb_raw", tag="wb_raw", align_bytes=64)
+        nc.gpsimd.dma_start(wb_raw[:].bitcast(I32), wb_words[0].bitcast(I32))
+        wbs_raw = keep.tile([P, N], U8, name="wbs_raw", align_bytes=64)
         nc.vector.memset(wbs_raw[:].bitcast(I32), 0)
         for q in range(QUADS):
             nc.sync.dma_start(wbs_raw[32 * q : 32 * q + 4, :].bitcast(I32), wb_scales[0, 4 * q : 4 * q + 4, :].bitcast(I32))
+        places = keep.tile([P, G // 16], U16, name="places")
+        nc.sync.dma_start(places[:], offs2)
         old_rows = old.rearrange("(p t) c -> p t c", t=PACK)
         old_sb = []
         for h in range(2):
-            half = keep.tile([P, 2, C], F32, name=f"old{h}", tag=("w_raw", "ws_raw")[h], align_bytes=64)
-            nc.sync.dma_start(half[:], old_rows[:, 2 * h : 2 * h + 2, :])
-            old_sb.append(half)
+            part = keep.tile([P, PACK, C // 2], F32, name=f"old{h}", tag=f"xw_win{h}", align_bytes=64)
+            nc.sync.dma_start(part[:], old_rows[:, :, h * C // 2 : (h + 1) * C // 2])
+            old_sb.append(part)
 
-        hid = keep.tile([P, G, PACK], BF16, name="hid", align_bytes=64)
-        for h in range(2):
-            bank = psum.tile([P, 2, J], F32, name=f"a{h}")
-            for u in range(2):
-                t = 2 * h + u
-                for z in range(PASSES):
+        hid = keep.tile([P, G, PACK], BF16, name="hid", tag="hid", align_bytes=64)
+        for h, slots in ((0, slice(0, J)), (1, slice(0, J // 2)), (1, slice(J // 2, J))):
+            width = slots.stop - slots.start
+            bank = psum.tile([P, 2, width], F32, name=f"a{h}_{slots.start}")
+            for z in range(PASSES):
+                cols = slice(z * J + slots.start, z * J + slots.stop)
+                for u in range(2):
                     nc.tensor.matmul_mx(
                         out=bank[:, u, :],
-                        lhsT=w_dealt[:, z, t, :].bitcast(E4M3X4),
-                        lhsT_scale=ws_dealt[:, z, t, :],
-                        rhs=xw_got[:, z * J : (z + 1) * J].bitcast(E5M2X4),
-                        rhs_scale=xs_plane[:, z * J : (z + 1) * J],
-                        start=(z == 0),
-                        stop=(z == PASSES - 1),
+                        lhsT=w_dealt[:, z, 2 * h + u, :].bitcast(E4M3X4),
+                        lhsT_scale=ws_dealt[:, z, 2 * h + u, :],
+                        rhs=xw_got[:, cols].bitcast(E5M2X4),
+                        rhs_scale=xs_plane[:, cols],
+                        start=(z == 0 and u == 0),
+                        stop=(z == PASSES - 1 and u == 1),
                     )
             nc.vector.tensor_reduce(
-                hid[:, :, 2 * h : 2 * h + 2],
+                hid[:, slots.start // 2 : slots.stop // 2, 2 * h : 2 * h + 2],
                 bank[:].rearrange("p u (g two) -> p g u two", two=2),
                 axis=mybir.AxisListType.X,
                 op=ALU.max,
             )
 
-        wb_dealt = keep.tile([P, PACK, 2 * P], U8, name="wb_dealt", align_bytes=64)
+        wb_dealt = keep.tile([P, PACK, 2 * P], U8, name="wb_dealt", tag="w_raw", align_bytes=64)
         nc.vector.tensor_copy(
             wb_dealt[:].bitcast(U16).rearrange("p t m -> p m t"),
             wb_raw[:].bitcast(U16).rearrange("p (m t) -> p m t", t=PACK),
         )
-        wbs_dealt = keep.tile([P, PACK, P], U8, name="wbs_dealt", align_bytes=64)
+        wbs_dealt = keep.tile([P, PACK, P], U8, name="wbs_dealt", tag="ws_raw", align_bytes=64)
         nc.vector.tensor_copy(
             wbs_dealt[:].rearrange("p t m -> p m t"), wbs_raw[:].rearrange("p (m t) -> p m t", t=PACK)
         )
 
-        pages = [keep.tile([P, C], F32, name=f"page{t}", tag=("page0", "page1", "page2", "xs_got")[t], align_bytes=64) for t in range(PACK)]
-        for t in range(PACK):
-            nc.vector.memset(pages[t][:].bitcast(I32), 0)
+        pages = [keep.tile([P, C], F32, name="page0", align_bytes=64)]
+        nc.vector.memset(pages[0][:], 0.0)
 
-        hid_words = keep.tile([P, G], U32, name="hid_words", align_bytes=64)
+        hid_words = keep.tile([P, G], U32, name="hid_words", tag="hid_words", align_bytes=64)
         hid_plane = keep.tile([P, G], U8, name="hid_plane", align_bytes=64)
         nc.vector.quantize_mx(
             out=hid_words[:].bitcast(E5M2X4), scales=hid_plane[:], in_=hid[:].rearrange("p g t -> p (g t)")
         )
 
+        p_sb = []
         for t in range(PACK):
             bank = psum.tile([P, G], F32, name=f"p{t}")
             nc.tensor.matmul_mx(
@@ -144,47 +141,66 @@ def tile_list_headpicks_pooled_scattered_pl_kernel(
                 start=True,
                 stop=True,
             )
-            p_sb = keep.tile([P, G], F32, name=f"p_sb{t}")
-            if t == 0:
-                nc.vector.tensor_copy(p_sb[:], bank[:])
-                nc.vector.tensor_copy(pages[t][:].indirect(places[:]), p_sb[:])
+            rows = keep.tile([P, G], F32, name=f"p_sb{t}")
+            p_sb.append(rows)
+            if t < 2:
+                nc.vector.tensor_copy(rows[:], bank[:])
             else:
-                nc.scalar.activation(p_sb[:], bank[:], COPY)
-                nc.scalar.activation(pages[t][:].indirect(places[:]), p_sb[:], COPY)
+                nc.scalar.activation(rows[:], bank[:], COPY)
+        for tag in ("wb_raw", "hid", "hid_words"):
+            page = keep.tile([P, C], F32, name=f"page_on_{tag}", tag=tag, align_bytes=64)
+            nc.gpsimd.memset(page[:], 0.0)
+            pages.append(page)
+        nc.vector.tensor_copy(pages[0][:].indirect(places[:]), p_sb[0][:])
+        for t in range(1, PACK):
+            nc.scalar.activation(pages[t][:].indirect(places[:]), p_sb[t][:], COPY)
 
-        y = keep.tile([P, PACK, C], F32, name="y", align_bytes=64)
+        half = C // 2
+        y = keep.tile([P, 2, PACK, half], F32, name="y", align_bytes=64)
         y_rows = out_0.rearrange("(p t) c -> p t c", t=PACK)
 
-        def add_old(t, cols):
+        def add_old(t, c0, c1):
             nc.vector.scalar_tensor_tensor(
-                out=y[:, t, cols], in0=old_sb[t // 2][:, t % 2, cols], scalar=0.5, in1=pages[t][:, cols],
-                op0=ALU.mult, op1=ALU.add,
+                out=y[:, c0 // half, t, c0 % half : c0 % half + c1 - c0],
+                in0=old_sb[c0 // half][:, t, c0 % half : c0 % half + c1 - c0],
+                scalar=0.5,
+                in1=pages[t][:, c0:c1],
+                op0=ALU.mult,
+                op1=ALU.add,
             )
 
-        for t in range(2):
-            add_old(t, slice(0, C))
-            nc.sync.dma_start(y_rows[:, t, :], y[:, t, :])
+        for h in range(2):
+            for t in range(PACK):
+                step = CHUNK if t == PACK - 1 else half
+                for c0 in range(h * half, (h + 1) * half, step):
+                    add_old(t, c0, c0 + step)
+                nc.sync.dma_start(y_rows[:, t, h * half : (h + 1) * half], y[:, h, t, :])
 
         y_words = keep.tile([P, C], U32, name="y_words", align_bytes=64)
         y_plane = keep.tile([P, C], U8, name="y_plane", align_bytes=64)
         words_out = out_1[0].rearrange("p c r -> p (c r)").bitcast(I32)
-        chunks = [slice(c, c + CHUNK) for c in range(0, C, CHUNK)]
-        for cols in chunks:
-            for t in range(2, PACK):
-                add_old(t, cols)
-            nc.sync.dma_start(y_rows[:, 2:PACK, cols], y[:, 2:PACK, cols])
-        for i, cols in enumerate(chunks):
-            y16 = keep.tile([P, CHUNK, PACK], BF16, name=f"y16_{i}", align_bytes=64)
-            dst = y16[:].rearrange("p (c i) t -> p c t i", i=4)
-            src = y[:, :, cols].rearrange("p t (c i) -> p c t i", i=4)
-            if i in ROUND_ON_VECTOR:
-                nc.vector.tensor_copy(dst, src)
-            else:
-                nc.scalar.copy(dst, src)
-            nc.vector.quantize_mx(
-                out=y_words[:, cols].bitcast(E4M3X4), scales=y_plane[:, cols], in_=y16[:].rearrange("p c t -> p (c t)")
+        y16 = keep.tile([P, C, PACK], BF16, name="y16", align_bytes=64)
+
+        def round_cols(copy, c0):
+            copy(
+                y16[:, c0 : c0 + CHUNK, :].rearrange("p (c i) t -> p c t i", i=4),
+                y[:, c0 // half, :, c0 % half : c0 % half + CHUNK].rearrange("p t (c i) -> p c t i", i=4),
             )
-            nc.sync.dma_start(words_out[:, cols], y_words[:, cols].bitcast(I32))
+
+        def quantise(c0, c1):
+            nc.vector.quantize_mx(
+                out=y_words[:, c0:c1].bitcast(E4M3X4),
+                scales=y_plane[:, c0:c1],
+                in_=y16[:, c0:c1, :].rearrange("p c t -> p (c t)"),
+            )
+            nc.sync.dma_start(words_out[:, c0:c1], y_words[:, c0:c1].bitcast(I32))
+
+        for k in range(3):
+            round_cols(nc.scalar.copy, k * CHUNK)
+        quantise(0, half)
+        round_cols(nc.vector.tensor_copy, 3 * CHUNK)
+        quantise(2 * CHUNK, 3 * CHUNK)
+        quantise(3 * CHUNK, C)
         for q in range(QUADS):
-            queue = nc.sync if q % 2 == 0 else nc.scalar
+            queue = nc.sync if q < 2 else nc.scalar
             queue.dma_start(out_2[0, 4 * q : 4 * q + 4, :].bitcast(I32), y_plane[32 * q : 32 * q + 4, :].bitcast(I32))

@@ -72,8 +72,8 @@ def tile_list_headpicks_pooled_scattered_pl_kernel(
                     dealt[:, z].rearrange("p t m -> p m t"), raw[:, z].rearrange("p (m t) -> p m t", t=PACK)
                 )
 
-        wb_raw = keep.tile([P, 2 * N], U8, name="wb_raw", tag="wb_raw", align_bytes=64)
-        nc.gpsimd.dma_start(wb_raw[:].bitcast(I32), wb_words[0].bitcast(I32))
+        wb_raw = keep.tile([P, 2 * N], U8, name="wb_raw", align_bytes=64)
+        nc.sync.dma_start(wb_raw[:].bitcast(I32), wb_words[0].bitcast(I32))
         wbs_raw = keep.tile([P, N], U8, name="wbs_raw", align_bytes=64)
         nc.vector.memset(wbs_raw[:].bitcast(I32), 0)
         for q in range(QUADS):
@@ -120,8 +120,9 @@ def tile_list_headpicks_pooled_scattered_pl_kernel(
             wbs_dealt[:].rearrange("p t m -> p m t"), wbs_raw[:].rearrange("p (m t) -> p m t", t=PACK)
         )
 
-        pages = [keep.tile([P, C], F32, name="page0", align_bytes=64)]
-        nc.vector.memset(pages[0][:], 0.0)
+        pages = [keep.tile([P, C], F32, name=f"page{t}", align_bytes=64) for t in range(2)]
+        for page in pages:
+            nc.vector.memset(page[:].bitcast(I32), 0)
 
         hid_words = keep.tile([P, G], U32, name="hid_words", tag="hid_words", align_bytes=64)
         hid_plane = keep.tile([P, G], U8, name="hid_plane", align_bytes=64)
@@ -147,7 +148,7 @@ def tile_list_headpicks_pooled_scattered_pl_kernel(
                 nc.vector.tensor_copy(rows[:], bank[:])
             else:
                 nc.scalar.activation(rows[:], bank[:], COPY)
-        for tag in ("wb_raw", "hid", "hid_words"):
+        for tag in ("hid", "hid_words"):
             page = keep.tile([P, C], F32, name=f"page_on_{tag}", tag=tag, align_bytes=64)
             nc.gpsimd.memset(page[:], 0.0)
             pages.append(page)
@@ -171,10 +172,14 @@ def tile_list_headpicks_pooled_scattered_pl_kernel(
 
         for h in range(2):
             for t in range(PACK):
-                step = CHUNK if t == PACK - 1 else half
+                first = h == 0 and t == 0
+                step = CHUNK if first or t == PACK - 1 else half
                 for c0 in range(h * half, (h + 1) * half, step):
                     add_old(t, c0, c0 + step)
-                nc.sync.dma_start(y_rows[:, t, h * half : (h + 1) * half], y[:, h, t, :])
+                    if first:
+                        nc.sync.dma_start(y_rows[:, t, c0 : c0 + step], y[:, h, t, c0 : c0 + step])
+                if not first:
+                    nc.sync.dma_start(y_rows[:, t, h * half : (h + 1) * half], y[:, h, t, :])
 
         y_words = keep.tile([P, C], U32, name="y_words", align_bytes=64)
         y_plane = keep.tile([P, C], U8, name="y_plane", align_bytes=64)

@@ -152,7 +152,9 @@ def tile_list_headpicks_pooled_scattered_pl_kernel(
             page = keep.tile([P, C], F32, name=f"page_on_{tag}", tag=tag, align_bytes=64)
             nc.gpsimd.memset(page[:], 0.0)
             pages.append(page)
-        nc.vector.tensor_copy(pages[0][:].indirect(places[:]), p_sb[0][:])
+        zeros = keep.tile([P, G], F32, name="zeros", align_bytes=64)
+        nc.vector.memset(zeros[:], 0.0)
+        nc.vector.tensor_tensor(pages[0][:].indirect(places[:]), p_sb[0][:], zeros[:], ALU.add)
         for t in range(1, PACK):
             nc.scalar.activation(pages[t][:].indirect(places[:]), p_sb[t][:], COPY)
 

from contextlib import ExitStack

import concourse.mybir as mybir

K, T, J, R, G, N, C = 1024, 512, 256, 512, 128, 512, 1024
FLOPS = 2 * K * R * J + 2 * R * N * G

F32 = mybir.dt.float32
BF16 = mybir.dt.bfloat16
I32 = mybir.dt.int32
U32 = mybir.dt.uint32
U16 = mybir.dt.uint16
U8 = mybir.dt.uint8
E4M3X4 = mybir.dt.float8_e4m3fn_x4
E5M2X4 = mybir.dt.float8_e5m2_x4
E2M1X4 = mybir.dt.float4_e2m1fn_x4
ALU = mybir.AluOpType
COPY = mybir.ActivationFunctionType.Copy

P = 128
PACK = 4
PASSES = K // (P * PACK)
QUADS = 4
CHUNK = 256


def tile_list_headpicks_pooled_scattered_pl_kernel(
    tc, xt_words, xt_scales, w_words, w_scales, wb_words, wb_scales, old, offs, offs2, out_0, out_1, out_2
):
    nc = tc.nc
    with ExitStack() as ctx:
        keep = ctx.enter_context(tc.tile_pool(name="keep", bufs=1))
        psum = ctx.enter_context(tc.psum_pool(name="psum", bufs=1))

        picks = keep.tile([P, J // 16], U16, name="picks")
        nc.sync.dma_start(picks[:], offs)

        xs_win = [keep.tile([P, T], U8, name=f"xs_win{z}", tag=f"xs_win{z}", align_bytes=64) for z in range(PASSES)]
        for z in range(PASSES):
            nc.vector.memset(xs_win[z][:].bitcast(I32), 0)
            nc.sync.dma_start(xs_win[z][0:P:8, :].bitcast(I32), xt_scales[z].bitcast(I32))
        xw_win = [keep.tile([P, T], U32, name=f"xw_win{z}", tag=f"xw_win{z}", align_bytes=64) for z in range(PASSES)]
        for z in range(PASSES):
            nc.sync.dma_start(xw_win[z][:].bitcast(I32), xt_words[z].rearrange("p c r -> p (c r)").bitcast(I32))
        w_raw = keep.tile([P, PASSES, R], I32, name="w_raw", tag="w_raw", align_bytes=64)
        nc.sync.dma_start(w_raw[:], w_words.rearrange("z p c r -> p z (c r)").bitcast(I32))
        ws_raw = keep.tile([P, PASSES, R], U8, name="ws_raw", tag="ws_raw", align_bytes=64)
        nc.vector.memset(ws_raw[:].bitcast(I32), 0)
        for q in range(QUADS):
            nc.scalar.dma_start(
                ws_raw[32 * q : 32 * q + 4].bitcast(I32),
                w_scales[:, 4 * q : 4 * q + 4, :].rearrange("z r c -> r z c").bitcast(I32),
            )

        xs_plane = keep.tile([P, PASSES * J], U8, name="xs_plane", align_bytes=64)
        nc.vector.memset(xs_plane[:].bitcast(I32), 0)

        xs_got = keep.tile([P, PASSES * J], U8, name="xs_got", tag="xs_got", align_bytes=64)
        for z in range(PASSES):
            nc.vector.tensor_copy(xs_got[:, z * J : (z + 1) * J], xs_win[z][:].indirect(picks[:]))
        for r in range(4):
            queue = nc.sync if r % 2 == 0 else nc.scalar
            queue.dma_start(xs_plane[r:P:32, :].bitcast(I32), xs_got[8 * r : P : 32, :].bitcast(I32))

        xw_got = keep.tile([P, PASSES * J], U32, name="xw_got", tag="xs_win1", align_bytes=64)
        w_dealt = keep.tile([P, PASSES, PACK, P], I32, name="w_dealt", align_bytes=64)
        ws_dealt = keep.tile([P, PASSES, PACK, P], U8, name="ws_dealt", align_bytes=64)
        for z in range(PASSES):
            nc.vector.tensor_copy(xw_got[:, z * J : (z + 1) * J], xw_win[z][:].indirect(picks[:]))
            for dealt, raw in ((w_dealt, w_raw), (ws_dealt, ws_raw)):
                nc.vector.tensor_copy(
                    dealt[:, z].rearrange("p t m -> p m t"), raw[:, z].rearrange("p (m t) -> p m t", t=PACK)
                )

        wb_raw = keep.tile([P, 2 * N], U8, name="wb_raw", align_bytes=64)
        nc.sync.dma_start(wb_raw[:].bitcast(I32), wb_words[0].bitcast(I32))
        wbs_raw = keep.tile([P, N], U8, name="wbs_raw", align_bytes=64)
        nc.vector.memset(wbs_raw[:].bitcast(I32), 0)
        for q in range(QUADS):
            nc.sync.dma_start(wbs_raw[32 * q : 32 * q + 4, :].bitcast(I32), wb_scales[0, 4 * q : 4 * q + 4, :].bitcast(I32))
        places = keep.tile([P, G // 16], U16, name="places")
        nc.sync.dma_start(places[:], offs2)
        old_rows = old.rearrange("(p t) c -> p t c", t=PACK)
        old_sb = []
        for h in range(2):
            part = keep.tile([P, PACK, C // 2], F32, name=f"old{h}", tag=f"xw_win{h}", align_bytes=64)
            nc.sync.dma_start(part[:], old_rows[:, :, h * C // 2 : (h + 1) * C // 2])
            old_sb.append(part)

        hid = keep.tile([P, G, PACK], BF16, name="hid", tag="hid", align_bytes=64)
        for h, slots in ((0, slice(0, J)), (1, slice(0, J // 2)), (1, slice(J // 2, J))):
            width = slots.stop - slots.start
            bank = psum.tile([P, 2, width], F32, name=f"a{h}_{slots.start}")
            for z in range(PASSES):
                cols = slice(z * J + slots.start, z * J + slots.stop)
                for u in range(2):
                    nc.tensor.matmul_mx(
                        out=bank[:, u, :],
                        lhsT=w_dealt[:, z, 2 * h + u, :].bitcast(E4M3X4),
                        lhsT_scale=ws_dealt[:, z, 2 * h + u, :],
                        rhs=xw_got[:, cols].bitcast(E5M2X4),
                        rhs_scale=xs_plane[:, cols],
                        start=(z == 0 and u == 0),
                        stop=(z == PASSES - 1 and u == 1),
                    )
            nc.vector.tensor_reduce(
                hid[:, slots.start // 2 : slots.stop // 2, 2 * h : 2 * h + 2],
                bank[:].rearrange("p u (g two) -> p g u two", two=2),
                axis=mybir.AxisListType.X,
                op=ALU.max,
            )

        wb_dealt = keep.tile([P, PACK, 2 * P], U8, name="wb_dealt", tag="w_raw", align_bytes=64)
        nc.vector.tensor_copy(
            wb_dealt[:].bitcast(U16).rearrange("p t m -> p m t"),
            wb_raw[:].bitcast(U16).rearrange("p (m t) -> p m t", t=PACK),
        )
        wbs_dealt = keep.tile([P, PACK, P], U8, name="wbs_dealt", tag="ws_raw", align_bytes=64)
        nc.vector.tensor_copy(
            wbs_dealt[:].rearrange("p t m -> p m t"), wbs_raw[:].rearrange("p (m t) -> p m t", t=PACK)
        )

        pages = [keep.tile([P, C], F32, name=f"page{t}", align_bytes=64) for t in range(2)]
        for page in pages:
            nc.vector.memset(page[:].bitcast(I32), 0)

        hid_words = keep.tile([P, G], U32, name="hid_words", tag="hid_words", align_bytes=64)
        hid_plane = keep.tile([P, G], U8, name="hid_plane", align_bytes=64)
        nc.vector.quantize_mx(
            out=hid_words[:].bitcast(E5M2X4), scales=hid_plane[:], in_=hid[:].rearrange("p g t -> p (g t)")
        )

        p_sb = []
        for t in range(PACK):
            bank = psum.tile([P, G], F32, name=f"p{t}")
            nc.tensor.matmul_mx(
                out=bank[:],
                lhsT=wb_dealt[:, t, :].bitcast(E2M1X4),
                lhsT_scale=wbs_dealt[:, t, :],
                rhs=hid_words[:].bitcast(E5M2X4),
                rhs_scale=hid_plane[:],
                start=True,
                stop=True,
            )
            rows = keep.tile([P, G], F32, name=f"p_sb{t}")
            p_sb.append(rows)
            if t < 2:
                nc.vector.tensor_copy(rows[:], bank[:])
            else:
                nc.scalar.activation(rows[:], bank[:], COPY)
        for tag in ("hid", "hid_words"):
            page = keep.tile([P, C], F32, name=f"page_on_{tag}", tag=tag, align_bytes=64)
            nc.gpsimd.memset(page[:], 0.0)
            pages.append(page)
        zeros = keep.tile([P, G], F32, name="zeros", align_bytes=64)
        nc.vector.memset(zeros[:], 0.0)
        nc.vector.tensor_tensor(pages[0][:].indirect(places[:]), p_sb[0][:], zeros[:], ALU.add)
        for t in range(1, PACK):
            nc.scalar.activation(pages[t][:].indirect(places[:]), p_sb[t][:], COPY)

        half = C // 2
        y = keep.tile([P, 2, PACK, half], F32, name="y", align_bytes=64)
        y_rows = out_0.rearrange("(p t) c -> p t c", t=PACK)

        def add_old(t, c0, c1):
            nc.vector.scalar_tensor_tensor(
                out=y[:, c0 // half, t, c0 % half : c0 % half + c1 - c0],
                in0=old_sb[c0 // half][:, t, c0 % half : c0 % half + c1 - c0],
                scalar=0.5,
                in1=pages[t][:, c0:c1],
                op0=ALU.mult,
                op1=ALU.add,
            )

        for h in range(2):
            for t in range(PACK):
                first = h == 0 and t == 0
                step = CHUNK if first or t == PACK - 1 else half
                for c0 in range(h * half, (h + 1) * half, step):
                    add_old(t, c0, c0 + step)
                    if first:
                        nc.sync.dma_start(y_rows[:, t, c0 : c0 + step], y[:, h, t, c0 : c0 + step])
                if not first:
                    nc.sync.dma_start(y_rows[:, t, h * half : (h + 1) * half], y[:, h, t, :])

        y_words = keep.tile([P, C], U32, name="y_words", align_bytes=64)
        y_plane = keep.tile([P, C], U8, name="y_plane", align_bytes=64)
        words_out = out_1[0].rearrange("p c r -> p (c r)").bitcast(I32)
        y16 = keep.tile([P, C, PACK], BF16, name="y16", align_bytes=64)

        def round_cols(copy, c0):
            copy(
                y16[:, c0 : c0 + CHUNK, :].rearrange("p (c i) t -> p c t i", i=4),
                y[:, c0 // half, :, c0 % half : c0 % half + CHUNK].rearrange("p t (c i) -> p c t i", i=4),
            )

        def quantise(c0, c1):
            nc.vector.quantize_mx(
                out=y_words[:, c0:c1].bitcast(E4M3X4),
                scales=y_plane[:, c0:c1],
                in_=y16[:, c0:c1, :].rearrange("p c t -> p (c t)"),
            )
            nc.sync.dma_start(words_out[:, c0:c1], y_words[:, c0:c1].bitcast(I32))

        for k in range(3):
            round_cols(nc.scalar.copy, k * CHUNK)
        quantise(0, half)
        round_cols(nc.vector.tensor_copy, 3 * CHUNK)
        quantise(2 * CHUNK, 3 * CHUNK)
        quantise(3 * CHUNK, C)
        for q in range(QUADS):
            queue = nc.sync if q < 2 else nc.scalar
            queue.dma_start(out_2[0, 4 * q : 4 * q + 4, :].bitcast(I32), y_plane[32 * q : 32 * q + 4, :].bitcast(I32))
